import numpy as np
import ml_dtypes


def mxq(x, axis, fmt="e4m3"):
    dtype, down = {"e4m3": (ml_dtypes.float8_e4m3fn, 7), "e5m2": (ml_dtypes.float8_e5m2, 14)}[fmt]
    v = np.moveaxis(np.asarray(x, np.float32).astype(ml_dtypes.bfloat16).astype(np.float64), axis, -1)
    blocks = v.reshape(v.shape[:-1] + (-1, 32))
    amax = np.abs(blocks).max(-1, keepdims=True)
    byte = np.maximum(np.where(amax > 0, np.frexp(amax)[1] - 1 + 127, 0) - down, 1)
    scale = np.exp2(byte - 127.0)
    codes = (blocks / scale).astype(np.float32).astype(dtype).astype(np.float64)
    return np.moveaxis((codes * scale).reshape(v.shape), -1, axis)


WIDE = False


def mx_kscale(k):
    if not WIDE:
        return np.ones(k)
    levels = np.array([10, -10, 5, -5, 0])
    if k % 512:
        return np.exp2(np.random.permutation(np.resize(levels, k // 32))).repeat(32)
    a = np.empty((k // 512, 16))
    for p in range(k // 512):
        a[p, :8] = np.random.permutation(np.resize(levels, 8))
        for g in range(8):
            far = levels[np.abs(levels - a[p, g]) >= 10]
            a[p, g + 8] = far[np.random.randint(len(far))]
    return np.exp2(a.ravel()).repeat(32)


BF16 = ml_dtypes.bfloat16


def bf(x):
    return np.asarray(x, np.float32).astype(BF16)


def f64(x):
    return np.asarray(x).astype(np.float64)

E4M3FN = np.array([(-1.0 if i & 128 else 1.0) * ((1.0 + (i & 7) / 8.0) * 2.0 ** (((i >> 3) & 15) - 7) if i & 120 else (i & 7) * 2.0 ** -9) for i in range(256)])


def e4m3fn_bytes(y):
    return np.clip(np.asarray(y, np.float64), -448.0, 448.0).astype(np.float32).astype(ml_dtypes.float8_e4m3fn).view(np.uint8)


def e4m3fn_values(b):
    return E4M3FN[b]

def planes(Y):
    n, m = Y.shape
    b = f64(bf(Y)).reshape(n // 32, 32, m)
    amax = np.abs(b).max(1)
    byte = np.clip(np.where(amax > 0, np.frexp(amax)[1] - 1 + 127 - 7, 1), 1, 254)
    codes = (b * np.exp2(127.0 - byte)[:, None, :]).reshape(n, m).astype(np.float32).astype(ml_dtypes.float8_e4m3fn).view(np.uint8)
    words = codes.reshape(n // 512, 128, 4, m).transpose(0, 1, 3, 2)
    return np.ascontiguousarray(words), np.ascontiguousarray(byte.astype(np.uint8).reshape(n // 512, 16, m))


T, K, D, B = 2048, 1536, 1024, 128

def setup_inputs():
    s = mx_kscale(K)
    X = np.random.randn(T, K) * np.repeat(np.exp(0.5 * np.random.randn(T, K // B)), B, axis=1)
    X = X / np.sqrt(np.mean(X * X, axis=1, keepdims=True)) * np.random.uniform(0.7, 1.0, (T, 1))
    X = X * s[None, :]
    block = np.abs(X).reshape(T, K // B, B).max(axis=2) / 448.0
    X_rscale = np.float32(block.max(axis=1, keepdims=True) / 448.0)
    X_sbytes = np.maximum(e4m3fn_bytes(block / f64(X_rscale)), np.uint8(1))
    step = e4m3fn_values(X_sbytes) * f64(X_rscale)
    X_bytes = e4m3fn_bytes(X / np.repeat(step, B, axis=1))
    W = 0.29 * np.random.randn(K, D) / np.sqrt(K) / s[:, None]
    phase = np.pi * (np.random.rand(1, D) - 0.5)
    side = np.where(np.random.rand(1, D) < 0.5, -1.0, 1.0)
    amp = np.sqrt(2.0) * side * np.exp(0.2 * np.random.randn(1, D))
    root_w = np.exp(0.8 * np.random.randn(T, 1))
    return {"X_bytes": X_bytes, "X_sbytes": X_sbytes, "X_rscale": X_rscale,
            "W": bf(W), "phase": bf(phase), "amp": bf(amp), "root_w": bf(root_w)}

def reference(X_bytes, X_sbytes, X_rscale, W, phase, amp, root_w):
    X = e4m3fn_values(X_bytes) * np.repeat(e4m3fn_values(X_sbytes), B, axis=1) * f64(X_rscale)
    U = mxq(X, 1, "e4m3") @ mxq(f64(W), 0, "e4m3")
    Z = f64(amp) * np.cos(U + f64(phase))
    y = f64(root_w) * Z
    words, scales = planes(y)
    return y, words, scales

@@ -1,0 +1,369 @@
+import math
+from contextlib import ExitStack
+
+import concourse.mybir as mybir
+from concourse.masks import make_identity
+
+T, K, D, B = 2048, 1536, 1024, 128
+FLOPS = 2 * T * K * D
+
+F32 = mybir.dt.float32
+BF16 = mybir.dt.bfloat16
+U32 = mybir.dt.uint32
+I32 = mybir.dt.int32
+U8 = mybir.dt.uint8
+FP8 = mybir.dt.float8_e4m3fn
+FP8X4 = mybir.dt.float8_e4m3fn_x4
+ACT = mybir.ActivationFunctionType
+MULT = mybir.AluOpType.mult
+
+P = 128
+PACK = 4
+SPAN = P * PACK
+GROUPS = T // SPAN
+PASSES = K // SPAN
+TILES = D // P
+STEPS = GROUPS * TILES
+BLOCKS = K // B
+QUARTER = 256
+QUARTERS = D // QUARTER
+X_ITEMS = 2 * PASSES
+
+UNIT_TILES = [4, 4, 4, 4, 4, 4, 2, 2, 2, 1, 1]
+COS_BUFS = 10
+RUN = 1
+TURN_LAG = 2
+ROUND_LAG = 2
+CATCH_TURN = 24
+CATCH_ROUND = 24
+XQ_LAG = 0
+W_START = -1
+Y_ON_SCALAR = [s for s in range(STEPS) if s % 4 == 3]
+Y_BUFS = 5
+U_BANKS = 3
+Y_BANKS = 3
+X_START = 0
+WIDEN_LEAD = 1
+W_ON_SCALAR = [(0, 0), (0, 1), (1, 0), (2, 0), (3, 0)]
+
+
+def tile_weighted_fourier_features_b14_kernel(tc, X_bytes, X_sbytes, X_rscale, W, phase, amp, root_w, out_0, out_1, out_2):
+    nc = tc.nc
+    x_rows = X_bytes.rearrange("(g p t) k -> g p t k", p=P, t=PACK)
+    w_rows = W.rearrange("(c p j) n -> c p j n", p=P, j=PACK)
+    y_rows = out_0.rearrange("(g p t) m -> g p t m", p=P, t=PACK)
+    y_words = out_1.rearrange("g p m t -> g p (m t)").bitcast(I32)
+    y_scale_rows = out_2.bitcast(I32)
+
+    units = []
+    unit_of_step = []
+    for n_tiles in UNIT_TILES:
+        units.append((len(unit_of_step), n_tiles))
+        unit_of_step.extend([len(units) - 1] * n_tiles)
+
+    with ExitStack() as ctx:
+        keep = ctx.enter_context(tc.tile_pool(name="keep", bufs=1))
+        work = ctx.enter_context(tc.tile_pool(name="work", bufs=3))
+        psum = ctx.enter_context(tc.psum_pool(name="psum", bufs=3))
+        ctx.enter_context(tc.manual_schedule())
+
+        sbytes = keep.tile([P, GROUPS, 64], U8, name="sbytes")
+        rscale = keep.tile([P, GROUPS, PACK], F32, name="rscale")
+        rootw = keep.tile([P, GROUPS, PACK], BF16, name="rootw")
+        phase_rows = keep.tile([TILES, P], BF16, name="phase_rows")
+        amp_all = keep.tile([P, D], BF16, name="amp_all")
+        xbytes = {}
+        w_raw = {}
+
+        def load_x(g, pair):
+            xbytes[g, pair] = keep.tile([P, 2, K], U8, name="xbytes%d_%d" % (g, pair))
+            nc.sync.dma_start(out=xbytes[g, pair][:], in_=x_rows[g, :, 2 * pair : 2 * pair + 2, :])
+
+        def load_w(c, first, count):
+            raw = keep.tile([P, PACK, count * QUARTER], BF16, name="wraw%d_%d" % (c, first))
+            nc.sync.dma_start(out=raw[:], in_=w_rows[c, :, :, first * QUARTER : (first + count) * QUARTER])
+            for q in range(count):
+                w_raw[first + q, c] = raw[:, :, q * QUARTER : (q + 1) * QUARTER]
+
+        nc.sync.dma_start(out=sbytes[:, :, : PACK * BLOCKS], in_=X_sbytes.rearrange("(g p t) b -> p g (t b)", p=P, t=PACK))
+        nc.sync.dma_start(out=rscale[:], in_=X_rscale.rearrange("(g p t) o -> p g (t o)", p=P, t=PACK))
+        load_x(0, 0)
+        load_w(0, 0, 1)
+        load_x(0, 1)
+        load_w(1, 0, 1)
+        load_w(2, 0, 1)
+        nc.sync.dma_start(out=phase_rows[:], in_=phase.rearrange("o (j p) -> (o j) p", p=P))
+        for c in range(PASSES):
+            load_w(c, 1, 1)
+        load_x(1, 0)
+        for c in range(PASSES):
+            load_w(c, 2, 2)
+        load_x(1, 1)
+        nc.sync.dma_start(out=rootw[:], in_=root_w.rearrange("(g p t) o -> p g (t o)", p=P, t=PACK))
+        nc.sync.dma_start(out=amp_all[:], in_=amp.rearrange("o n -> (o n)").partition_broadcast(P))
+        for g in range(2, GROUPS):
+            load_x(g, 0)
+            load_x(g, 1)
+
+        ident = keep.tile([P, P], F32, name="ident")
+        make_identity(nc, ident[:])
+        phase_f32 = keep.tile([P, P], F32, name="phase_f32")
+        nc.gpsimd.memset(phase_f32[:], 0.0)
+        warm = keep.tile([P, 1], F32, name="warm")
+        nc.scalar.activation(out=warm[:], in_=phase_f32[:, 0:1], func=ACT.Sin)
+
+        svalue = keep.tile([P, GROUPS * PACK, BLOCKS], F32, name="svalue")
+        xscale = keep.tile([P, GROUPS * PACK, BLOCKS], F32, name="xscale")
+        for g in range(GROUPS):
+            nc.vector.tensor_copy(
+                out=svalue[:, PACK * g : PACK * (g + 1), :].rearrange("p r b -> p (r b)"),
+                in_=sbytes[:, g, : PACK * BLOCKS].bitcast(FP8),
+            )
+        nc.vector.tensor_tensor(
+            out=xscale[:],
+            in0=svalue[:],
+            in1=rscale[:].rearrange("p g t -> p (g t)").unsqueeze(2).to_broadcast([P, GROUPS * PACK, BLOCKS]),
+            op=MULT,
+        )
+        phase_col = keep.tile([P, TILES], F32, name="phase_col")
+
+        def make_phase_column():
+            nc.scalar.copy(out=phase_f32[0:TILES, :], in_=phase_rows[:])
+            bank = psum.tile([P, P], F32, name="phase_bank", tag="x_bank", bufs=2)
+            nc.tensor.transpose(out=bank[:], in_=phase_f32[:], identity=ident[:])
+            nc.scalar.copy(out=phase_col[:], in_=bank[:, 0:TILES])
+
+        w_grouped, w_codes, w_scales = {}, {}, {}
+
+        def interleave_w(q, c):
+            grouped = work.tile([P, QUARTER, PACK], BF16, name="w_grouped", bufs=4, align_bytes=64)
+            w_grouped[q, c] = grouped
+            dst = grouped[:].rearrange("p (a i) j -> p a j i", i=4)
+            src = w_raw[q, c].rearrange("p j (a i) -> p a j i", i=4)
+            if (q, c) in W_ON_SCALAR:
+                nc.scalar.copy(out=dst, in_=src)
+            else:
+                nc.vector.tensor_copy(out=dst, in_=src)
+
+        def quantize_w(q, c):
+            w_codes[q, c] = keep.tile([P, QUARTER], U32, name="wcodes%d_%d" % (q, c), align_bytes=64)
+            w_scales[q, c] = keep.tile([P, QUARTER], U8, name="wscales%d_%d" % (q, c), align_bytes=64)
+            nc.vector.quantize_mx(
+                out=w_codes[q, c][:].bitcast(FP8X4),
+                scales=w_scales[q, c][:],
+                in_=w_grouped[q, c][:].rearrange("p n j -> p (n j)"),
+            )
+
+        x_wide, x_bank, x_grouped, x_codes, x_scales = {}, {}, {}, {}, {}
+
+        def widen_x(g, item):
+            pair, c = divmod(item, PASSES)
+            wide = work.tile([P, 2, SPAN], BF16, name="x_wide", bufs=WIDEN_LEAD + 3)
+            x_wide[g, item] = wide
+            for tt in range(2):
+                sorted_view = wide[:, tt, :].rearrange("r (u p e) -> r p u e", u=2, e=2)
+                for b in range(SPAN // B):
+                    block = c * (SPAN // B) + b
+                    src = xbytes[g, pair][:, tt, block * B : (block + 1) * B].bitcast(FP8)
+                    nc.vector.tensor_scalar(
+                        out=sorted_view[:, 32 * b : 32 * (b + 1)],
+                        in0=src.rearrange("r (p u e) -> r p u e", u=2, e=2),
+                        scalar1=xscale[:, PACK * g + 2 * pair + tt, block : block + 1],
+                        scalar2=None,
+                        op0=MULT,
+                    )
+
+        def transpose_x(g, item):
+            bank = psum.tile([P, 2, 2, P], F32, name="x_bank", tag="x_bank", bufs=2)
+            x_bank[g, item] = bank
+            words = x_wide[g, item][:].rearrange("r t k -> r (t k)").bitcast(F32)
+            for tt in range(2):
+                for u in range(2):
+                    first = (2 * tt + u) * P
+                    nc.tensor.transpose(out=bank[:, tt, u, :], in_=words[:, first : first + P], identity=ident[:])
+
+        def copy_out_x(g, item):
+            pair, c = divmod(item, PASSES)
+            if pair == 0:
+                x_grouped[g, c] = work.tile([P, SPAN, 2], F32, name="x_grouped", bufs=4, align_bytes=64)
+            dst = x_grouped[g, c][:, 2 * P * pair : 2 * P * (pair + 1), :].rearrange("p (t r) u -> p t r u", t=2)
+            nc.scalar.copy(out=dst, in_=x_bank[g, item][:].rearrange("p t u r -> p t r u"))
+
+        def quantize_x(g, c):
+            x_codes[g, c] = work.tile([P, SPAN], U32, name="x_codes", bufs=2 * PASSES + 1, align_bytes=64)
+            x_scales[g, c] = work.tile([P, SPAN], U8, name="x_scales", bufs=2 * PASSES + 1, align_bytes=64)
+            nc.vector.quantize_mx(
+                out=x_codes[g, c][:].bitcast(FP8X4),
+                scales=x_scales[g, c][:],
+                in_=x_grouped[g, c][:].rearrange("p r u -> p (r u)").bitcast(BF16),
+            )
+
+        u_bank, folded, cosine, y_bank, y_tile, y_grouped, y_scales = {}, {}, {}, {}, {}, {}, {}
+
+        def multiply(s):
+            g, j = divmod(s, TILES)
+            q, half = divmod(j, QUARTER // P)
+            cols = slice(half * P, (half + 1) * P)
+            u_bank[s] = psum.tile([P, SPAN], F32, name="u_bank", bufs=U_BANKS)
+            for c in range(PASSES):
+                nc.tensor.matmul_mx(
+                    out=u_bank[s][:],
+                    lhsT=w_codes[q, c][:, cols].bitcast(FP8X4),
+                    lhsT_scale=w_scales[q, c][:, cols],
+                    rhs=x_codes[g, c][:].bitcast(FP8X4),
+                    rhs_scale=x_scales[g, c][:],
+                    start=(c == 0),
+                    stop=(c == PASSES - 1),
+                )
+
+        def fold(s):
+            j = s % TILES
+            folded[s] = work.tile([P, SPAN], F32, name="folded")
+            nc.scalar.activation(out=folded[s][:], in_=u_bank[s][:], func=ACT.Abs, bias=phase_col[:, j : j + 1])
+
+        def take_cosine(s):
+            cosine[s] = work.tile([P, SPAN], F32, name="cosine", bufs=COS_BUFS)
+            nc.scalar.activation(out=cosine[s][:], in_=folded[s][:], func=ACT.Sin, scale=-1.0, bias=math.pi / 2)
+
+        def transpose_y(s):
+            first, n_tiles = units[unit_of_step[s]]
+            per_bank = PACK // n_tiles
+            y_bank[s] = psum.tile([P, per_bank, n_tiles, P], F32, name="y_bank", bufs=Y_BANKS)
+            for i in range(per_bank):
+                t = (s - first) * per_bank + i
+                for j in range(n_tiles):
+                    nc.tensor.transpose(out=y_bank[s][:, i, j, :], in_=cosine[first + j][:, t * P : (t + 1) * P], identity=ident[:])
+
+        def columns(unit):
+            first, n_tiles = units[unit]
+            return first // TILES, slice((first % TILES) * P, (first % TILES + n_tiles) * P)
+
+        def weigh(s):
+            unit = unit_of_step[s]
+            first, n_tiles = units[unit]
+            g, cols = columns(unit)
+            per_bank = PACK // n_tiles
+            if s == first:
+                y_tile[unit] = work.tile([P, PACK, n_tiles * P], F32, name="y_tile", bufs=Y_BUFS)
+            for i in range(per_bank):
+                t = (s - first) * per_bank + i
+                nc.vector.scalar_tensor_tensor(
+                    out=y_tile[unit][:, t, :],
+                    in0=y_bank[s][:, i].rearrange("p j m -> p (j m)"),
+                    scalar=rootw[:, g, t : t + 1],
+                    in1=amp_all[:, cols],
+                    op0=MULT,
+                    op1=MULT,
+                )
+            if s == first + n_tiles - 1:
+                nc.sync.dma_start(out=y_rows[g, :, :, cols], in_=y_tile[unit][:])
+
+        def interleave_y(s):
+            unit = unit_of_step[s]
+            first, n_tiles = units[unit]
+            if s == first:
+                y_grouped[unit] = work.tile([P, n_tiles * P, PACK], BF16, name="y_grouped", align_bytes=64)
+            cols = slice((s - first) * P, (s - first + 1) * P)
+            dst = y_grouped[unit][:, cols, :].rearrange("p (a i) t -> p a t i", i=4)
+            src = y_tile[unit][:, :, cols].rearrange("p t (a i) -> p a t i", i=4)
+            if s in Y_ON_SCALAR:
+                nc.scalar.copy(out=dst, in_=src)
+            else:
+                nc.vector.tensor_copy(out=dst, in_=src)
+
+        def quantize_y(unit):
+            first, n_tiles = units[unit]
+            g, cols = columns(unit)
+            if first % TILES == 0:
+                y_scales[g] = work.tile([P, D], U8, name="y_scales", bufs=2, align_bytes=64)
+            codes = work.tile([P, n_tiles * P], U32, name="y_codes", align_bytes=64)
+            nc.vector.quantize_mx(
+                out=codes[:].bitcast(FP8X4),
+                scales=y_scales[g][:, cols],
+                in_=y_grouped[unit][:].rearrange("p m t -> p (m t)"),
+            )
+            nc.sync.dma_start(out=y_words[g, :, cols], in_=codes[:].bitcast(I32))
+            if (first + n_tiles) % TILES == 0:
+                rows = y_scales[g][:].bitcast(I32)
+                for quad in range(4):
+                    nc.sync.dma_start(out=y_scale_rows[g, 4 * quad : 4 * quad + 4, :], in_=rows[32 * quad : 32 * quad + 4, :])
+
+        def x_item(slot):
+            g, item = divmod(slot - X_START, TILES)
+            return (g + 1, item) if 0 <= g < GROUPS - 1 and item < X_ITEMS else None
+
+        def w_items(slot):
+            return [(q, c) for q in range(1, QUARTERS) for c in range(PASSES) if (2 * (PASSES * (q - 1) + c)) // PASSES + W_START == slot]
+
+        def last_of_unit(s):
+            return 0 <= s < STEPS and s == sum(units[unit_of_step[s]]) - 1
+
+        interleave_w(0, 0)
+        for item in range(X_ITEMS):
+            widen_x(0, item)
+            transpose_x(0, item)
+            copy_out_x(0, item)
+            if item == 1:
+                interleave_w(0, 1)
+        interleave_w(0, 2)
+        for c in range(PASSES):
+            quantize_w(0, c)
+        for c in range(PASSES):
+            quantize_x(0, c)
+        make_phase_column()
+
+        def steps(first):
+            return [s for s in range(first, first + RUN) if 0 <= s < STEPS]
+
+        def x_items(first):
+            return [x_item(s) for s in range(first, first + RUN) if x_item(s)]
+
+        def queue_slots(ready, catch_up):
+            slots = []
+            for s in range(STEPS):
+                slot = max([ready(s)] + slots[-1:])
+                while slots.count(slot) >= (2 if slot >= catch_up else 1):
+                    slot += 1
+                slots.append(slot)
+            return slots
+
+        def unit_end(s):
+            return sum(units[unit_of_step[s]]) - 1
+
+        turn_slot = queue_slots(lambda s: unit_end(s) + TURN_LAG, CATCH_TURN)
+        round_slot = queue_slots(lambda s: turn_slot[unit_end(s)] + ROUND_LAG, CATCH_ROUND)
+
+        def due(slot, slots):
+            return [s for s in range(STEPS) if slot <= slots[s] < slot + RUN]
+
+        for slot in range(-WIDEN_LEAD, round_slot[-1] + 2 * RUN, RUN):
+            for s in steps(slot):
+                multiply(s)
+            for item in x_items(slot - RUN):
+                copy_out_x(*item)
+            for s in due(slot - RUN, turn_slot):
+                weigh(s)
+            for s in due(slot, turn_slot):
+                transpose_y(s)
+            for item in x_items(slot):
+                transpose_x(*item)
+            for s in steps(slot - RUN):
+                take_cosine(s)
+            for s in range(slot, slot + RUN):
+                for w in w_items(s - RUN):
+                    quantize_w(*w)
+            for item in x_items(slot + WIDEN_LEAD):
+                widen_x(*item)
+            for s in due(slot - RUN, round_slot):
+                if last_of_unit(s):
+                    quantize_y(unit_of_step[s])
+            for g, item in x_items(slot - RUN - XQ_LAG):
+                if item >= PASSES:
+                    quantize_x(g, item - PASSES)
+            for s in steps(slot):
+                fold(s)
+            for s in range(slot, slot + RUN):
+                for w in w_items(s):
+                    interleave_w(*w)
+            for s in due(slot, round_slot):
+                interleave_y(s)

@@ -23,28 +23,20 @@ SPAN = P * PACK
 GROUPS = T // SPAN
 PASSES = K // SPAN
 TILES = D // P
-STEPS = GROUPS * TILES
 BLOCKS = K // B
 QUARTER = 256
 QUARTERS = D // QUARTER
+STEPS = GROUPS * QUARTERS
 X_ITEMS = 2 * PASSES
 
-UNIT_TILES = [4, 4, 4, 4, 4, 4, 2, 2, 2, 1, 1]
-COS_BUFS = 10
-RUN = 1
-TURN_LAG = 2
-ROUND_LAG = 2
-CATCH_TURN = 24
-CATCH_ROUND = 24
-XQ_LAG = 0
-W_START = -1
-Y_ON_SCALAR = [s for s in range(STEPS) if s % 4 == 3]
-Y_BUFS = 5
 U_BANKS = 3
-Y_BANKS = 3
-X_START = 0
-WIDEN_LEAD = 1
+T_BANKS = 5
+Y_BUFS = 8
+CATCH = 12
+ROOM = [1, 1, 1, 0]
+Y_LAG = 4
 W_ON_SCALAR = [(0, 0), (0, 1), (1, 0), (2, 0), (3, 0)]
+Y_ON_SCALAR = [0] * 12 + [256, 128, 256, 96]
 
 
 def tile_weighted_fourier_features_b14_kernel(tc, X_bytes, X_sbytes, X_rscale, W, phase, amp, root_w, out_0, out_1, out_2):
@@ -54,12 +46,6 @@ def tile_weighted_fourier_features_b14_kernel(tc, X_bytes, X_sbytes, X_rscale, W
     y_rows = out_0.rearrange("(g p t) m -> g p t m", p=P, t=PACK)
     y_words = out_1.rearrange("g p m t -> g p (m t)").bitcast(I32)
     y_scale_rows = out_2.bitcast(I32)
-
-    units = []
-    unit_of_step = []
-    for n_tiles in UNIT_TILES:
-        units.append((len(unit_of_step), n_tiles))
-        unit_of_step.extend([len(units) - 1] * n_tiles)
 
     with ExitStack() as ctx:
         keep = ctx.enter_context(tc.tile_pool(name="keep", bufs=1))
@@ -128,8 +114,7 @@ def tile_weighted_fourier_features_b14_kernel(tc, X_bytes, X_sbytes, X_rscale, W
         phase_col = keep.tile([P, TILES], F32, name="phase_col")
 
         def make_phase_column():
-            nc.scalar.copy(out=phase_f32[0:TILES, :], in_=phase_rows[:])
-            bank = psum.tile([P, P], F32, name="phase_bank", tag="x_bank", bufs=2)
+            bank = psum.tile([P, P], F32, name="phase_bank", tag="t_bank", bufs=T_BANKS)
             nc.tensor.transpose(out=bank[:], in_=phase_f32[:], identity=ident[:])
             nc.scalar.copy(out=phase_col[:], in_=bank[:, 0:TILES])
 
@@ -158,7 +143,7 @@ def tile_weighted_fourier_features_b14_kernel(tc, X_bytes, X_sbytes, X_rscale, W
 
         def widen_x(g, item):
             pair, c = divmod(item, PASSES)
-            wide = work.tile([P, 2, SPAN], BF16, name="x_wide", bufs=WIDEN_LEAD + 3)
+            wide = work.tile([P, 2, SPAN], BF16, name="x_wide", bufs=5)
             x_wide[g, item] = wide
             for tt in range(2):
                 sorted_view = wide[:, tt, :].rearrange("r (u p e) -> r p u e", u=2, e=2)
@@ -174,7 +159,7 @@ def tile_weighted_fourier_features_b14_kernel(tc, X_bytes, X_sbytes, X_rscale, W
                     )
 
         def transpose_x(g, item):
-            bank = psum.tile([P, 2, 2, P], F32, name="x_bank", tag="x_bank", bufs=2)
+            bank = psum.tile([P, 2, 2, P], F32, name="x_bank", tag="t_bank", bufs=T_BANKS)
             x_bank[g, item] = bank
             words = x_wide[g, item][:].rearrange("r t k -> r (t k)").bitcast(F32)
             for tt in range(2):
@@ -200,103 +185,90 @@ def tile_weighted_fourier_features_b14_kernel(tc, X_bytes, X_sbytes, X_rscale, W
 
         u_bank, folded, cosine, y_bank, y_tile, y_grouped, y_scales = {}, {}, {}, {}, {}, {}, {}
 
-        def multiply(s):
-            g, j = divmod(s, TILES)
-            q, half = divmod(j, QUARTER // P)
-            cols = slice(half * P, (half + 1) * P)
-            u_bank[s] = psum.tile([P, SPAN], F32, name="u_bank", bufs=U_BANKS)
-            for c in range(PASSES):
-                nc.tensor.matmul_mx(
-                    out=u_bank[s][:],
-                    lhsT=w_codes[q, c][:, cols].bitcast(FP8X4),
-                    lhsT_scale=w_scales[q, c][:, cols],
-                    rhs=x_codes[g, c][:].bitcast(FP8X4),
-                    rhs_scale=x_scales[g, c][:],
-                    start=(c == 0),
-                    stop=(c == PASSES - 1),
-                )
+        def multiply(n):
+            g, q = divmod(n, QUARTERS)
+            for j in range(2):
+                cols = slice(j * P, (j + 1) * P)
+                u_bank[n, j] = psum.tile([P, SPAN], F32, name="u_bank", bufs=U_BANKS)
+                for c in range(PASSES):
+                    nc.tensor.matmul_mx(
+                        out=u_bank[n, j][:],
+                        lhsT=w_codes[q, c][:, cols].bitcast(FP8X4),
+                        lhsT_scale=w_scales[q, c][:, cols],
+                        rhs=x_codes[g, c][:].bitcast(FP8X4),
+                        rhs_scale=x_scales[g, c][:],
+                        start=(c == 0),
+                        stop=(c == PASSES - 1),
+                    )
 
-        def fold(s):
-            j = s % TILES
-            folded[s] = work.tile([P, SPAN], F32, name="folded")
-            nc.scalar.activation(out=folded[s][:], in_=u_bank[s][:], func=ACT.Abs, bias=phase_col[:, j : j + 1])
+        def fold(n):
+            folded[n] = work.tile([P, 2, SPAN], F32, name="folded", bufs=2)
+            for j in range(2):
+                tile = 2 * (n % QUARTERS) + j
+                nc.scalar.activation(out=folded[n][:, j, :], in_=u_bank[n, j][:], func=ACT.Abs, bias=phase_col[:, tile : tile + 1])
 
-        def take_cosine(s):
-            cosine[s] = work.tile([P, SPAN], F32, name="cosine", bufs=COS_BUFS)
-            nc.scalar.activation(out=cosine[s][:], in_=folded[s][:], func=ACT.Sin, scale=-1.0, bias=math.pi / 2)
+        def take_cosine(n):
+            cosine[n] = work.tile([P, 2, SPAN], F32, name="cosine")
+            nc.scalar.activation(out=cosine[n][:], in_=folded[n][:], func=ACT.Sin, scale=-1.0, bias=math.pi / 2)
 
-        def transpose_y(s):
-            first, n_tiles = units[unit_of_step[s]]
-            per_bank = PACK // n_tiles
-            y_bank[s] = psum.tile([P, per_bank, n_tiles, P], F32, name="y_bank", bufs=Y_BANKS)
-            for i in range(per_bank):
-                t = (s - first) * per_bank + i
-                for j in range(n_tiles):
-                    nc.tensor.transpose(out=y_bank[s][:, i, j, :], in_=cosine[first + j][:, t * P : (t + 1) * P], identity=ident[:])
+        def transpose_y(n):
+            for pair in range(2):
+                y_bank[n, pair] = psum.tile([P, 2, 2, P], F32, name="y_bank", tag="t_bank", bufs=T_BANKS)
+                for tt in range(2):
+                    t = 2 * pair + tt
+                    for j in range(2):
+                        nc.tensor.transpose(out=y_bank[n, pair][:, tt, j, :], in_=cosine[n][:, j, t * P : (t + 1) * P], identity=ident[:])
 
-        def columns(unit):
-            first, n_tiles = units[unit]
-            return first // TILES, slice((first % TILES) * P, (first % TILES + n_tiles) * P)
+        def weigh(n):
+            g, q = divmod(n, QUARTERS)
+            cols = slice(q * QUARTER, (q + 1) * QUARTER)
+            y_tile[n] = work.tile([P, PACK, QUARTER], F32, name="y_tile", bufs=Y_BUFS)
+            for pair in range(2):
+                for tt in range(2):
+                    t = 2 * pair + tt
+                    nc.vector.scalar_tensor_tensor(
+                        out=y_tile[n][:, t, :],
+                        in0=y_bank[n, pair][:, tt].rearrange("p j m -> p (j m)"),
+                        scalar=rootw[:, g, t : t + 1],
+                        in1=amp_all[:, cols],
+                        op0=MULT,
+                        op1=MULT,
+                    )
+            nc.sync.dma_start(out=y_rows[g, :, :, cols], in_=y_tile[n][:])
 
-        def weigh(s):
-            unit = unit_of_step[s]
-            first, n_tiles = units[unit]
-            g, cols = columns(unit)
-            per_bank = PACK // n_tiles
-            if s == first:
-                y_tile[unit] = work.tile([P, PACK, n_tiles * P], F32, name="y_tile", bufs=Y_BUFS)
-            for i in range(per_bank):
-                t = (s - first) * per_bank + i
-                nc.vector.scalar_tensor_tensor(
-                    out=y_tile[unit][:, t, :],
-                    in0=y_bank[s][:, i].rearrange("p j m -> p (j m)"),
-                    scalar=rootw[:, g, t : t + 1],
-                    in1=amp_all[:, cols],
-                    op0=MULT,
-                    op1=MULT,
-                )
-            if s == first + n_tiles - 1:
-                nc.sync.dma_start(out=y_rows[g, :, :, cols], in_=y_tile[unit][:])
+        def interleave_y(n):
+            y_grouped[n] = work.tile([P, QUARTER, PACK], BF16, name="y_grouped", bufs=4, align_bytes=64)
+            dst = y_grouped[n][:].rearrange("p (a i) t -> p a t i", i=4)
+            src = y_tile[n][:].rearrange("p t (a i) -> p a t i", i=4)
+            cut = Y_ON_SCALAR[n] // 4
+            if cut > 0:
+                nc.scalar.copy(out=dst[:, :cut], in_=src[:, :cut])
+            if cut < QUARTER // 4:
+                nc.vector.tensor_copy(out=dst[:, cut:], in_=src[:, cut:])
 
-        def interleave_y(s):
-            unit = unit_of_step[s]
-            first, n_tiles = units[unit]
-            if s == first:
-                y_grouped[unit] = work.tile([P, n_tiles * P, PACK], BF16, name="y_grouped", align_bytes=64)
-            cols = slice((s - first) * P, (s - first + 1) * P)
-            dst = y_grouped[unit][:, cols, :].rearrange("p (a i) t -> p a t i", i=4)
-            src = y_tile[unit][:, :, cols].rearrange("p t (a i) -> p a t i", i=4)
-            if s in Y_ON_SCALAR:
-                nc.scalar.copy(out=dst, in_=src)
-            else:
-                nc.vector.tensor_copy(out=dst, in_=src)
-
-        def quantize_y(unit):
-            first, n_tiles = units[unit]
-            g, cols = columns(unit)
-            if first % TILES == 0:
+        def quantize_y(n):
+            g, q = divmod(n, QUARTERS)
+            cols = slice(q * QUARTER, (q + 1) * QUARTER)
+            if q == 0:
                 y_scales[g] = work.tile([P, D], U8, name="y_scales", bufs=2, align_bytes=64)
-            codes = work.tile([P, n_tiles * P], U32, name="y_codes", align_bytes=64)
+            codes = work.tile([P, QUARTER], U32, name="y_codes", bufs=4, align_bytes=64)
             nc.vector.quantize_mx(
                 out=codes[:].bitcast(FP8X4),
                 scales=y_scales[g][:, cols],
-                in_=y_grouped[unit][:].rearrange("p m t -> p (m t)"),
+                in_=y_grouped[n][:].rearrange("p m t -> p (m t)"),
             )
             nc.sync.dma_start(out=y_words[g, :, cols], in_=codes[:].bitcast(I32))
-            if (first + n_tiles) % TILES == 0:
+            if q == QUARTERS - 1:
                 rows = y_scales[g][:].bitcast(I32)
                 for quad in range(4):
                     nc.sync.dma_start(out=y_scale_rows[g, 4 * quad : 4 * quad + 4, :], in_=rows[32 * quad : 32 * quad + 4, :])
 
-        def x_item(slot):
-            g, item = divmod(slot - X_START, TILES)
-            return (g + 1, item) if 0 <= g < GROUPS - 1 and item < X_ITEMS else None
+        def x_items(n):
+            g, q = divmod(n, QUARTERS)
+            return [(g + 1, 2 * q), (g + 1, 2 * q + 1)] if 0 <= g < GROUPS - 1 and q < PASSES else []
 
-        def w_items(slot):
-            return [(q, c) for q in range(1, QUARTERS) for c in range(PASSES) if (2 * (PASSES * (q - 1) + c)) // PASSES + W_START == slot]
-
-        def last_of_unit(s):
-            return 0 <= s < STEPS and s == sum(units[unit_of_step[s]]) - 1
+        def w_items(n):
+            return [(n + 2, c) for c in range(PASSES)] if 1 <= n + 2 < QUARTERS else []
 
         interleave_w(0, 0)
         for item in range(X_ITEMS):
@@ -305,6 +277,8 @@ def tile_weighted_fourier_features_b14_kernel(tc, X_bytes, X_sbytes, X_rscale, W
             copy_out_x(0, item)
             if item == 1:
                 interleave_w(0, 1)
+            if item == 3:
+                nc.scalar.copy(out=phase_f32[0:TILES, :], in_=phase_rows[:])
         interleave_w(0, 2)
         for c in range(PASSES):
             quantize_w(0, c)
@@ -312,58 +286,39 @@ def tile_weighted_fourier_features_b14_kernel(tc, X_bytes, X_sbytes, X_rscale, W
             quantize_x(0, c)
         make_phase_column()
 
-        def steps(first):
-            return [s for s in range(first, first + RUN) if 0 <= s < STEPS]
+        def run(stage, n):
+            if 0 <= n < STEPS:
+                stage(n)
 
-        def x_items(first):
-            return [x_item(s) for s in range(first, first + RUN) if x_item(s)]
+        round_slot = []
+        for n in range(STEPS):
+            slot = max([n + Y_LAG] + round_slot[-1:])
+            while round_slot.count(slot) >= (2 if slot >= CATCH else ROOM[slot % QUARTERS]):
+                slot += 1
+            round_slot.append(slot)
 
-        def queue_slots(ready, catch_up):
-            slots = []
-            for s in range(STEPS):
-                slot = max([ready(s)] + slots[-1:])
-                while slots.count(slot) >= (2 if slot >= catch_up else 1):
-                    slot += 1
-                slots.append(slot)
-            return slots
-
-        def unit_end(s):
-            return sum(units[unit_of_step[s]]) - 1
-
-        turn_slot = queue_slots(lambda s: unit_end(s) + TURN_LAG, CATCH_TURN)
-        round_slot = queue_slots(lambda s: turn_slot[unit_end(s)] + ROUND_LAG, CATCH_ROUND)
-
-        def due(slot, slots):
-            return [s for s in range(STEPS) if slot <= slots[s] < slot + RUN]
-
-        for slot in range(-WIDEN_LEAD, round_slot[-1] + 2 * RUN, RUN):
-            for s in steps(slot):
-                multiply(s)
-            for item in x_items(slot - RUN):
+        for n in range(-1, round_slot[-1] + 2):
+            run(multiply, n)
+            for item in x_items(n - 1):
                 copy_out_x(*item)
-            for s in due(slot - RUN, turn_slot):
-                weigh(s)
-            for s in due(slot, turn_slot):
-                transpose_y(s)
-            for item in x_items(slot):
+            run(weigh, n - 3)
+            run(transpose_y, n - 2)
+            for item in x_items(n):
                 transpose_x(*item)
-            for s in steps(slot - RUN):
-                take_cosine(s)
-            for s in range(slot, slot + RUN):
-                for w in w_items(s - RUN):
-                    quantize_w(*w)
-            for item in x_items(slot + WIDEN_LEAD):
-                widen_x(*item)
-            for s in due(slot - RUN, round_slot):
-                if last_of_unit(s):
-                    quantize_y(unit_of_step[s])
-            for g, item in x_items(slot - RUN - XQ_LAG):
+            run(take_cosine, n - 1)
+            for w in w_items(n - 1):
+                quantize_w(*w)
+            for m in range(STEPS):
+                if round_slot[m] == n - 1:
+                    quantize_y(m)
+            run(fold, n)
+            for m in range(STEPS):
+                if round_slot[m] == n:
+                    interleave_y(m)
+            for g, item in x_items(n - 1):
                 if item >= PASSES:
                     quantize_x(g, item - PASSES)
-            for s in steps(slot):
-                fold(s)
-            for s in range(slot, slot + RUN):
-                for w in w_items(s):
-                    interleave_w(*w)
-            for s in due(slot, round_slot):
-                interleave_y(s)
+            for item in x_items(n + 1):
+                widen_x(*item)
+            for w in w_items(n):
+                interleave_w(*w)

@@ -31,12 +31,17 @@ X_ITEMS = 2 * PASSES
 
 U_BANKS = 3
 T_BANKS = 5
-Y_BUFS = 8
+Y_BUFS = 10
 CATCH = 12
 ROOM = [1, 1, 1, 0]
-Y_LAG = 4
+ROOM2 = 2
+Y_LAG = 3
 W_ON_SCALAR = [(0, 0), (0, 1), (1, 0), (2, 0), (3, 0)]
-Y_ON_SCALAR = [0] * 12 + [256, 128, 256, 96]
+G_STEPS = 15
+G_COLS = 128
+TAIL = {13: 128, 14: 128, 15: 96}
+EARLY = True
+LASTG = 0
 
 
 def tile_weighted_fourier_features_b14_kernel(tc, X_bytes, X_sbytes, X_rscale, W, phase, amp, root_w, out_0, out_1, out_2):
@@ -82,9 +87,10 @@ def tile_weighted_fourier_features_b14_kernel(tc, X_bytes, X_sbytes, X_rscale, W
         for c in range(PASSES):
             load_w(c, 1, 1)
         load_x(1, 0)
-        for c in range(PASSES):
-            load_w(c, 2, 2)
+        load_w(0, 2, 2)
         load_x(1, 1)
+        load_w(1, 2, 2)
+        load_w(2, 2, 2)
         nc.sync.dma_start(out=rootw[:], in_=root_w.rearrange("(g p t) o -> p g (t o)", p=P, t=PACK))
         nc.sync.dma_start(out=amp_all[:], in_=amp.rearrange("o n -> (o n)").partition_broadcast(P))
         for g in range(2, GROUPS):
@@ -98,19 +104,16 @@ def tile_weighted_fourier_features_b14_kernel(tc, X_bytes, X_sbytes, X_rscale, W
         warm = keep.tile([P, 1], F32, name="warm")
         nc.scalar.activation(out=warm[:], in_=phase_f32[:, 0:1], func=ACT.Sin)
 
-        svalue = keep.tile([P, GROUPS * PACK, BLOCKS], F32, name="svalue")
         xscale = keep.tile([P, GROUPS * PACK, BLOCKS], F32, name="xscale")
+
         for g in range(GROUPS):
-            nc.vector.tensor_copy(
-                out=svalue[:, PACK * g : PACK * (g + 1), :].rearrange("p r b -> p (r b)"),
-                in_=sbytes[:, g, : PACK * BLOCKS].bitcast(FP8),
-            )
-        nc.vector.tensor_tensor(
-            out=xscale[:],
-            in0=svalue[:],
-            in1=rscale[:].rearrange("p g t -> p (g t)").unsqueeze(2).to_broadcast([P, GROUPS * PACK, BLOCKS]),
-            op=MULT,
-        )
+            for t in range(PACK):
+                nc.scalar.activation(
+                    out=xscale[:, PACK * g + t, :],
+                    in_=sbytes[:, g, t * BLOCKS : (t + 1) * BLOCKS].bitcast(FP8),
+                    func=ACT.Copy,
+                    scale=rscale[:, g, t : t + 1],
+                )
         phase_col = keep.tile([P, TILES], F32, name="phase_col")
 
         def make_phase_column():
@@ -184,6 +187,7 @@ def tile_weighted_fourier_features_b14_kernel(tc, X_bytes, X_sbytes, X_rscale, W
             )
 
         u_bank, folded, cosine, y_bank, y_tile, y_grouped, y_scales = {}, {}, {}, {}, {}, {}, {}
+        y_side, y_codes, left = {}, {}, {}
 
         def multiply(n):
             g, q = divmod(n, QUARTERS)
@@ -209,7 +213,8 @@ def tile_weighted_fourier_features_b14_kernel(tc, X_bytes, X_sbytes, X_rscale, W
 
         def take_cosine(n):
             cosine[n] = work.tile([P, 2, SPAN], F32, name="cosine")
-            nc.scalar.activation(out=cosine[n][:], in_=folded[n][:], func=ACT.Sin, scale=-1.0, bias=math.pi / 2)
+            for part in ([slice(0, 2)] if x_items(n) else [slice(0, 1), slice(1, 2)]):
+                nc.scalar.activation(out=cosine[n][:, part], in_=folded[n][:, part], func=ACT.Sin, scale=-1.0, bias=math.pi / 2)
 
         def transpose_y(n):
             for pair in range(2):
@@ -234,34 +239,73 @@ def tile_weighted_fourier_features_b14_kernel(tc, X_bytes, X_sbytes, X_rscale, W
                         op0=MULT,
                         op1=MULT,
                     )
-            nc.sync.dma_start(out=y_rows[g, :, :, cols], in_=y_tile[n][:])
+                if n == STEPS - 1:
+                    rows = slice(2 * pair, 2 * pair + 2)
+                    nc.sync.dma_start(out=y_rows[g, :, rows, cols], in_=y_tile[n][:, rows, :])
+            if n < STEPS - 1:
+                nc.sync.dma_start(out=y_rows[g, :, :, cols], in_=y_tile[n][:])
+
+        def own_cols(n):
+            return QUARTER - G_COLS if n < G_STEPS else QUARTER
+
+        def open_planes(n):
+            g, q = divmod(n, QUARTERS)
+            if g not in y_scales:
+                y_scales[g] = keep.tile([P, D], U8, name="y_scales%d" % g, align_bytes=64)
+            if n not in y_codes:
+                y_codes[n] = work.tile([P, QUARTER], U32, name="y_codes", bufs=Y_BUFS, align_bytes=64)
+
+        def quantize_part(n, first, count, src):
+            g, q = divmod(n, QUARTERS)
+            open_planes(n)
+            nc.vector.quantize_mx(
+                out=y_codes[n][:, first : first + count].bitcast(FP8X4),
+                scales=y_scales[g][:, q * QUARTER + first : q * QUARTER + first + count],
+                in_=src[:].rearrange("p m t -> p (m t)"),
+            )
+            left[n] = left.get(n, QUARTER) - count
+            if left[n] == 0:
+                nc.sync.dma_start(out=y_words[g, :, q * QUARTER : (q + 1) * QUARTER], in_=y_codes[n][:].bitcast(I32))
+                if all(left.get(QUARTERS * g + i) == 0 for i in range(QUARTERS)):
+                    rows = y_scales[g][:].bitcast(I32)
+                    for quad in range(4):
+                        nc.sync.dma_start(out=y_scale_rows[g, 4 * quad : 4 * quad + 4, :], in_=rows[32 * quad : 32 * quad + 4, :])
+
+        def round_side(n):
+            if n < G_STEPS:
+                if n < STEPS - 1 - LASTG:
+                    y_side[n] = work.tile([P, G_COLS, PACK], BF16, name="y_side", bufs=1, align_bytes=64)
+                else:
+                    y_side[n] = work.tile([P, G_COLS, PACK], BF16, name="y_side_last", bufs=2, align_bytes=64)
+                (nc.gpsimd if n > 0 else nc.vector).tensor_scalar(
+                    out=y_side[n][:],
+                    in0=y_tile[n][:, :, QUARTER - G_COLS :].rearrange("p t m -> p m t"),
+                    scalar1=1.0,
+                    scalar2=0.0,
+                    op0=MULT,
+                    op1=mybir.AluOpType.add,
+                )
+
+        def quantize_side(n):
+            if n < G_STEPS:
+                quantize_part(n, QUARTER - G_COLS, G_COLS, y_side[n])
 
         def interleave_y(n):
-            y_grouped[n] = work.tile([P, QUARTER, PACK], BF16, name="y_grouped", bufs=4, align_bytes=64)
+            own = own_cols(n)
+            if own == 0:
+                return
+            y_grouped[n] = work.tile([P, own, PACK], BF16, name="y_grouped", bufs=4, align_bytes=64)
             dst = y_grouped[n][:].rearrange("p (a i) t -> p a t i", i=4)
-            src = y_tile[n][:].rearrange("p t (a i) -> p a t i", i=4)
-            cut = Y_ON_SCALAR[n] // 4
+            src = y_tile[n][:, :, :own].rearrange("p t (a i) -> p a t i", i=4)
+            cut = TAIL.get(n, 0) // 4
             if cut > 0:
                 nc.scalar.copy(out=dst[:, :cut], in_=src[:, :cut])
-            if cut < QUARTER // 4:
+            if cut < own // 4:
                 nc.vector.tensor_copy(out=dst[:, cut:], in_=src[:, cut:])
 
         def quantize_y(n):
-            g, q = divmod(n, QUARTERS)
-            cols = slice(q * QUARTER, (q + 1) * QUARTER)
-            if q == 0:
-                y_scales[g] = work.tile([P, D], U8, name="y_scales", bufs=2, align_bytes=64)
-            codes = work.tile([P, QUARTER], U32, name="y_codes", bufs=4, align_bytes=64)
-            nc.vector.quantize_mx(
-                out=codes[:].bitcast(FP8X4),
-                scales=y_scales[g][:, cols],
-                in_=y_grouped[n][:].rearrange("p m t -> p (m t)"),
-            )
-            nc.sync.dma_start(out=y_words[g, :, cols], in_=codes[:].bitcast(I32))
-            if q == QUARTERS - 1:
-                rows = y_scales[g][:].bitcast(I32)
-                for quad in range(4):
-                    nc.sync.dma_start(out=y_scale_rows[g, 4 * quad : 4 * quad + 4, :], in_=rows[32 * quad : 32 * quad + 4, :])
+            if own_cols(n) > 0:
+                quantize_part(n, 0, own_cols(n), y_grouped[n])
 
         def x_items(n):
             g, q = divmod(n, QUARTERS)
@@ -290,31 +334,33 @@ def tile_weighted_fourier_features_b14_kernel(tc, X_bytes, X_sbytes, X_rscale, W
             if 0 <= n < STEPS:
                 stage(n)
 
+        last = STEPS - 1
         round_slot = []
-        for n in range(STEPS):
+        for n in range(STEPS - 3):
             slot = max([n + Y_LAG] + round_slot[-1:])
-            while round_slot.count(slot) >= (2 if slot >= CATCH else ROOM[slot % QUARTERS]):
+            while round_slot.count(slot) >= (ROOM2 if slot >= CATCH else ROOM[slot % QUARTERS]):
                 slot += 1
             round_slot.append(slot)
+        assert round_slot[-1] <= last
 
-        for n in range(-1, round_slot[-1] + 2):
+        for n in range(-1, STEPS):
             run(multiply, n)
             for item in x_items(n - 1):
                 copy_out_x(*item)
             run(weigh, n - 3)
-            run(transpose_y, n - 2)
+            if not (EARLY and n == last):
+                run(transpose_y, n - 2)
             for item in x_items(n):
                 transpose_x(*item)
             run(take_cosine, n - 1)
+            if EARLY and n >= last - 1:
+                run(transpose_y, n - 1)
             for w in w_items(n - 1):
                 quantize_w(*w)
-            for m in range(STEPS):
-                if round_slot[m] == n - 1:
+            for m, slot in enumerate(round_slot):
+                if slot == n - 1:
                     quantize_y(m)
             run(fold, n)
-            for m in range(STEPS):
-                if round_slot[m] == n:
-                    interleave_y(m)
             for g, item in x_items(n - 1):
                 if item >= PASSES:
                     quantize_x(g, item - PASSES)
@@ -322,3 +368,44 @@ def tile_weighted_fourier_features_b14_kernel(tc, X_bytes, X_sbytes, X_rscale, W
                 widen_x(*item)
             for w in w_items(n):
                 interleave_w(*w)
+            rounds = [m for m, slot in enumerate(round_slot) if slot == n]
+            for m in rounds[:-1]:
+                interleave_y(m)
+            if n == 3:
+                round_side(0)
+            run(quantize_side, n - 4)
+            if n > 3:
+                run(round_side, n - 3)
+            for m in rounds[-1:]:
+                interleave_y(m)
+
+        take_cosine(last)
+        weigh(last - 2)
+        if EARLY:
+            for m, slot in enumerate(round_slot):
+                if slot == last:
+                    quantize_y(m)
+            quantize_side(last - 3)
+        round_side(last - 2)
+        if not EARLY:
+            transpose_y(last - 1)
+        weigh(last - 1)
+        transpose_y(last)
+        interleave_y(last - 2)
+        if EARLY:
+            quantize_side(last - 2)
+            quantize_y(last - 2)
+        round_side(last - 1)
+        weigh(last)
+        interleave_y(last - 1)
+        if not EARLY:
+            for m, slot in enumerate(round_slot):
+                if slot == last:
+                    quantize_y(m)
+            quantize_side(last - 3)
+            quantize_side(last - 2)
+            quantize_y(last - 2)
+        interleave_y(last)
+        quantize_side(last - 1)
+        quantize_y(last - 1)
+        quantize_y(last)

@@ -16,6 +16,7 @@ FP8 = mybir.dt.float8_e4m3fn
 FP8X4 = mybir.dt.float8_e4m3fn_x4
 ACT = mybir.ActivationFunctionType
 MULT = mybir.AluOpType.mult
+ADD = mybir.AluOpType.add
 
 P = 128
 PACK = 4
@@ -24,29 +25,25 @@ GROUPS = T // SPAN
 PASSES = K // SPAN
 TILES = D // P
 BLOCKS = K // B
-QUARTER = 256
+QUARTER = 2 * P
 QUARTERS = D // QUARTER
 STEPS = GROUPS * QUARTERS
+LAST = STEPS - 1
 X_ITEMS = 2 * PASSES
 
 U_BANKS = 3
 T_BANKS = 5
+WEIGH_LAG = 3
 Y_BUFS = 10
-CATCH = 12
-ROOM = [1, 1, 1, 0]
-ROOM2 = 2
-Y_LAG = 3
-W_ON_SCALAR = [(0, 0), (0, 1), (1, 0), (2, 0), (3, 0)]
-G_STEPS = 15
-G_COLS = 128
-TAIL = {13: 128, 14: 128, 15: 96}
-EARLY = True
-LASTG = 0
+HALF = QUARTER // 2
+LAST_ON_SCALAR = 96
 
 
 def tile_weighted_fourier_features_b14_kernel(tc, X_bytes, X_sbytes, X_rscale, W, phase, amp, root_w, out_0, out_1, out_2):
     nc = tc.nc
     x_rows = X_bytes.rearrange("(g p t) k -> g p t k", p=P, t=PACK)
+    sbyte_rows = X_sbytes.rearrange("(g p t) b -> p g (t b)", p=P, t=PACK)
+    rscale_rows = X_rscale.rearrange("(g p t) o -> p g (t o)", p=P, t=PACK)
     w_rows = W.rearrange("(c p j) n -> c p j n", p=P, j=PACK)
     y_rows = out_0.rearrange("(g p t) m -> g p t m", p=P, t=PACK)
     y_words = out_1.rearrange("g p m t -> g p (m t)").bitcast(I32)
@@ -58,63 +55,73 @@ def tile_weighted_fourier_features_b14_kernel(tc, X_bytes, X_sbytes, X_rscale, W
         psum = ctx.enter_context(tc.psum_pool(name="psum", bufs=3))
         ctx.enter_context(tc.manual_schedule())
 
-        sbytes = keep.tile([P, GROUPS, 64], U8, name="sbytes")
-        rscale = keep.tile([P, GROUPS, PACK], F32, name="rscale")
-        rootw = keep.tile([P, GROUPS, PACK], BF16, name="rootw")
-        phase_rows = keep.tile([TILES, P], BF16, name="phase_rows")
-        amp_all = keep.tile([P, D], BF16, name="amp_all")
-        xbytes = {}
-        w_raw = {}
+        sbytes, rscale, xbytes, w_raw = {}, {}, {}, {}
 
-        def load_x(g, pair):
-            xbytes[g, pair] = keep.tile([P, 2, K], U8, name="xbytes%d_%d" % (g, pair))
-            nc.sync.dma_start(out=xbytes[g, pair][:], in_=x_rows[g, :, 2 * pair : 2 * pair + 2, :])
+        def load_scales(first, count):
+            codes = keep.tile([P, count, 64], U8, name="sbytes%d" % first)
+            rows = keep.tile([P, count, 8], F32, name="rscale%d" % first)
+            nc.sync.dma_start(out=codes[:, :, : PACK * BLOCKS], in_=sbyte_rows[:, first : first + count])
+            nc.sync.dma_start(out=rows[:, :, :PACK], in_=rscale_rows[:, first : first + count])
+            for i in range(count):
+                sbytes[first + i] = codes[:, i, :]
+                rscale[first + i] = rows[:, i, :]
+
+        def load_x(g, first, count):
+            rows = keep.tile([P, count, K], U8, name="xbytes%d_%d" % (g, first))
+            nc.sync.dma_start(out=rows[:], in_=x_rows[g, :, first : first + count, :])
+            for i in range(count):
+                xbytes[g, first + i] = rows[:, i, :]
 
         def load_w(c, first, count):
             raw = keep.tile([P, PACK, count * QUARTER], BF16, name="wraw%d_%d" % (c, first))
             nc.sync.dma_start(out=raw[:], in_=w_rows[c, :, :, first * QUARTER : (first + count) * QUARTER])
-            for q in range(count):
-                w_raw[first + q, c] = raw[:, :, q * QUARTER : (q + 1) * QUARTER]
+            for i in range(count):
+                w_raw[first + i, c] = raw[:, :, i * QUARTER : (i + 1) * QUARTER]
 
-        nc.sync.dma_start(out=sbytes[:, :, : PACK * BLOCKS], in_=X_sbytes.rearrange("(g p t) b -> p g (t b)", p=P, t=PACK))
-        nc.sync.dma_start(out=rscale[:], in_=X_rscale.rearrange("(g p t) o -> p g (t o)", p=P, t=PACK))
-        load_x(0, 0)
+        rootw = keep.tile([P, GROUPS, PACK], BF16, name="rootw")
+        phase_rows = keep.tile([TILES, P], BF16, name="phase_rows")
+        amp_all = keep.tile([P, D], BF16, name="amp_all")
+
+        load_scales(0, 1)
+        load_x(0, 0, 1)
         load_w(0, 0, 1)
-        load_x(0, 1)
+        load_x(0, 1, 1)
+        load_x(0, 2, 2)
         load_w(1, 0, 1)
         load_w(2, 0, 1)
         nc.sync.dma_start(out=phase_rows[:], in_=phase.rearrange("o (j p) -> (o j) p", p=P))
+        load_scales(1, GROUPS - 1)
         for c in range(PASSES):
             load_w(c, 1, 1)
-        load_x(1, 0)
+        load_x(1, 0, 2)
         load_w(0, 2, 2)
-        load_x(1, 1)
+        load_x(1, 2, 2)
         load_w(1, 2, 2)
         load_w(2, 2, 2)
         nc.sync.dma_start(out=rootw[:], in_=root_w.rearrange("(g p t) o -> p g (t o)", p=P, t=PACK))
         nc.sync.dma_start(out=amp_all[:], in_=amp.rearrange("o n -> (o n)").partition_broadcast(P))
         for g in range(2, GROUPS):
-            load_x(g, 0)
-            load_x(g, 1)
+            load_x(g, 0, 2)
+            load_x(g, 2, 2)
 
         ident = keep.tile([P, P], F32, name="ident")
         make_identity(nc, ident[:])
         phase_f32 = keep.tile([P, P], F32, name="phase_f32")
         nc.gpsimd.memset(phase_f32[:], 0.0)
-        warm = keep.tile([P, 1], F32, name="warm")
-        nc.scalar.activation(out=warm[:], in_=phase_f32[:, 0:1], func=ACT.Sin)
+        table_preload = keep.tile([P, 1], F32, name="table_preload")
+        nc.scalar.activation(out=table_preload[:], in_=phase_f32[:, 0:1], func=ACT.Sin)
 
         xscale = keep.tile([P, GROUPS * PACK, BLOCKS], F32, name="xscale")
+        phase_col = keep.tile([P, TILES], F32, name="phase_col")
 
-        for g in range(GROUPS):
+        def combine_scales(g):
             for t in range(PACK):
                 nc.scalar.activation(
                     out=xscale[:, PACK * g + t, :],
-                    in_=sbytes[:, g, t * BLOCKS : (t + 1) * BLOCKS].bitcast(FP8),
+                    in_=sbytes[g][:, t * BLOCKS : (t + 1) * BLOCKS].bitcast(FP8),
                     func=ACT.Copy,
-                    scale=rscale[:, g, t : t + 1],
+                    scale=rscale[g][:, t : t + 1],
                 )
-        phase_col = keep.tile([P, TILES], F32, name="phase_col")
 
         def make_phase_column():
             bank = psum.tile([P, P], F32, name="phase_bank", tag="t_bank", bufs=T_BANKS)
@@ -124,11 +131,10 @@ def tile_weighted_fourier_features_b14_kernel(tc, X_bytes, X_sbytes, X_rscale, W
         w_grouped, w_codes, w_scales = {}, {}, {}
 
         def interleave_w(q, c):
-            grouped = work.tile([P, QUARTER, PACK], BF16, name="w_grouped", bufs=4, align_bytes=64)
-            w_grouped[q, c] = grouped
-            dst = grouped[:].rearrange("p (a i) j -> p a j i", i=4)
+            w_grouped[q, c] = work.tile([P, QUARTER, PACK], BF16, name="w_grouped", bufs=4, align_bytes=64)
+            dst = w_grouped[q, c][:].rearrange("p (a i) j -> p a j i", i=4)
             src = w_raw[q, c].rearrange("p j (a i) -> p a j i", i=4)
-            if (q, c) in W_ON_SCALAR:
+            if c == 0 or (q, c) == (0, 1):
                 nc.scalar.copy(out=dst, in_=src)
             else:
                 nc.vector.tensor_copy(out=dst, in_=src)
@@ -144,31 +150,29 @@ def tile_weighted_fourier_features_b14_kernel(tc, X_bytes, X_sbytes, X_rscale, W
 
         x_wide, x_bank, x_grouped, x_codes, x_scales = {}, {}, {}, {}, {}
 
-        def widen_x(g, item):
+        def widen_x(g, item, tt):
             pair, c = divmod(item, PASSES)
-            wide = work.tile([P, 2, SPAN], BF16, name="x_wide", bufs=5)
-            x_wide[g, item] = wide
-            for tt in range(2):
-                sorted_view = wide[:, tt, :].rearrange("r (u p e) -> r p u e", u=2, e=2)
-                for b in range(SPAN // B):
-                    block = c * (SPAN // B) + b
-                    src = xbytes[g, pair][:, tt, block * B : (block + 1) * B].bitcast(FP8)
-                    nc.vector.tensor_scalar(
-                        out=sorted_view[:, 32 * b : 32 * (b + 1)],
-                        in0=src.rearrange("r (p u e) -> r p u e", u=2, e=2),
-                        scalar1=xscale[:, PACK * g + 2 * pair + tt, block : block + 1],
-                        scalar2=None,
-                        op0=MULT,
-                    )
+            if tt == 0:
+                x_wide[g, item] = work.tile([P, 2, SPAN], BF16, name="x_wide", bufs=5)
+            sorted_view = x_wide[g, item][:, tt, :].rearrange("r (u p e) -> r p u e", u=2, e=2)
+            for b in range(SPAN // B):
+                block = c * (SPAN // B) + b
+                src = xbytes[g, 2 * pair + tt][:, block * B : (block + 1) * B].bitcast(FP8)
+                nc.vector.tensor_scalar(
+                    out=sorted_view[:, (B // PACK) * b : (B // PACK) * (b + 1)],
+                    in0=src.rearrange("r (p u e) -> r p u e", u=2, e=2),
+                    scalar1=xscale[:, PACK * g + 2 * pair + tt, block : block + 1],
+                    scalar2=None,
+                    op0=MULT,
+                )
 
         def transpose_x(g, item):
-            bank = psum.tile([P, 2, 2, P], F32, name="x_bank", tag="t_bank", bufs=T_BANKS)
-            x_bank[g, item] = bank
+            x_bank[g, item] = psum.tile([P, 2, 2, P], F32, name="x_bank", tag="t_bank", bufs=T_BANKS)
             words = x_wide[g, item][:].rearrange("r t k -> r (t k)").bitcast(F32)
             for tt in range(2):
                 for u in range(2):
                     first = (2 * tt + u) * P
-                    nc.tensor.transpose(out=bank[:, tt, u, :], in_=words[:, first : first + P], identity=ident[:])
+                    nc.tensor.transpose(out=x_bank[g, item][:, tt, u, :], in_=words[:, first : first + P], identity=ident[:])
 
         def copy_out_x(g, item):
             pair, c = divmod(item, PASSES)
@@ -186,8 +190,9 @@ def tile_weighted_fourier_features_b14_kernel(tc, X_bytes, X_sbytes, X_rscale, W
                 in_=x_grouped[g, c][:].rearrange("p r u -> p (r u)").bitcast(BF16),
             )
 
-        u_bank, folded, cosine, y_bank, y_tile, y_grouped, y_scales = {}, {}, {}, {}, {}, {}, {}
-        y_side, y_codes, left = {}, {}, {}
+        u_bank, folded, cosine, y_bank, y_tile = {}, {}, {}, {}, {}
+        whole = [slice(0, SPAN)]
+        by_pair = [slice(0, SPAN // 2), slice(SPAN // 2, SPAN)]
 
         def multiply(n):
             g, q = divmod(n, QUARTERS)
@@ -209,12 +214,19 @@ def tile_weighted_fourier_features_b14_kernel(tc, X_bytes, X_sbytes, X_rscale, W
             folded[n] = work.tile([P, 2, SPAN], F32, name="folded", bufs=2)
             for j in range(2):
                 tile = 2 * (n % QUARTERS) + j
-                nc.scalar.activation(out=folded[n][:, j, :], in_=u_bank[n, j][:], func=ACT.Abs, bias=phase_col[:, tile : tile + 1])
+                for part in by_pair if (n, j) == (LAST, 1) else whole:
+                    nc.scalar.activation(out=folded[n][:, j, part], in_=u_bank[n, j][:, part], func=ACT.Abs, bias=phase_col[:, tile : tile + 1])
 
         def take_cosine(n):
             cosine[n] = work.tile([P, 2, SPAN], F32, name="cosine")
-            for part in ([slice(0, 2)] if x_items(n) else [slice(0, 1), slice(1, 2)]):
-                nc.scalar.activation(out=cosine[n][:, part], in_=folded[n][:, part], func=ACT.Sin, scale=-1.0, bias=math.pi / 2)
+            if n == LAST:
+                pieces = [(slice(0, 2), part) for part in by_pair]
+            elif x_items(n):
+                pieces = [(slice(0, 2), slice(0, SPAN))]
+            else:
+                pieces = [(slice(j, j + 1), slice(0, SPAN)) for j in range(2)]
+            for tiles, part in pieces:
+                nc.scalar.activation(out=cosine[n][:, tiles, part], in_=folded[n][:, tiles, part], func=ACT.Sin, scale=-1.0, bias=math.pi / 2)
 
         def transpose_y(n):
             for pair in range(2):
@@ -239,73 +251,57 @@ def tile_weighted_fourier_features_b14_kernel(tc, X_bytes, X_sbytes, X_rscale, W
                         op0=MULT,
                         op1=MULT,
                     )
-                if n == STEPS - 1:
+                if n == LAST:
                     rows = slice(2 * pair, 2 * pair + 2)
                     nc.sync.dma_start(out=y_rows[g, :, rows, cols], in_=y_tile[n][:, rows, :])
-            if n < STEPS - 1:
+            if n < LAST:
                 nc.sync.dma_start(out=y_rows[g, :, :, cols], in_=y_tile[n][:])
 
-        def own_cols(n):
-            return QUARTER - G_COLS if n < G_STEPS else QUARTER
+        y_scales = keep.tile([P, D], U8, name="y_scales", align_bytes=64)
+        y_lower, y_upper, y_codes, features_left = {}, {}, {}, {}
 
-        def open_planes(n):
+        def quantize_features(n, first, count, rounded):
             g, q = divmod(n, QUARTERS)
-            if g not in y_scales:
-                y_scales[g] = keep.tile([P, D], U8, name="y_scales%d" % g, align_bytes=64)
             if n not in y_codes:
                 y_codes[n] = work.tile([P, QUARTER], U32, name="y_codes", bufs=Y_BUFS, align_bytes=64)
-
-        def quantize_part(n, first, count, src):
-            g, q = divmod(n, QUARTERS)
-            open_planes(n)
+                features_left[n] = QUARTER
             nc.vector.quantize_mx(
                 out=y_codes[n][:, first : first + count].bitcast(FP8X4),
-                scales=y_scales[g][:, q * QUARTER + first : q * QUARTER + first + count],
-                in_=src[:].rearrange("p m t -> p (m t)"),
+                scales=y_scales[PACK * g :, q * QUARTER + first : q * QUARTER + first + count],
+                in_=rounded[:].rearrange("p m t -> p (m t)"),
             )
-            left[n] = left.get(n, QUARTER) - count
-            if left[n] == 0:
+            features_left[n] = features_left[n] - count
+            if features_left[n] == 0:
                 nc.sync.dma_start(out=y_words[g, :, q * QUARTER : (q + 1) * QUARTER], in_=y_codes[n][:].bitcast(I32))
-                if all(left.get(QUARTERS * g + i) == 0 for i in range(QUARTERS)):
-                    rows = y_scales[g][:].bitcast(I32)
-                    for quad in range(4):
-                        nc.sync.dma_start(out=y_scale_rows[g, 4 * quad : 4 * quad + 4, :], in_=rows[32 * quad : 32 * quad + 4, :])
 
-        def round_side(n):
-            if n < G_STEPS:
-                if n < STEPS - 1 - LASTG:
-                    y_side[n] = work.tile([P, G_COLS, PACK], BF16, name="y_side", bufs=1, align_bytes=64)
-                else:
-                    y_side[n] = work.tile([P, G_COLS, PACK], BF16, name="y_side_last", bufs=2, align_bytes=64)
-                (nc.gpsimd if n > 0 else nc.vector).tensor_scalar(
-                    out=y_side[n][:],
-                    in0=y_tile[n][:, :, QUARTER - G_COLS :].rearrange("p t m -> p m t"),
-                    scalar1=1.0,
-                    scalar2=0.0,
-                    op0=MULT,
-                    op1=mybir.AluOpType.add,
-                )
+        def round_upper(n):
+            name = "y_upper" if n < LAST - 1 else "y_upper_end"
+            y_upper[n] = work.tile([P, HALF, PACK], BF16, name=name, bufs=1, align_bytes=64)
+            engine = nc.gpsimd if n > 0 else nc.vector
+            engine.tensor_scalar(
+                out=y_upper[n][:],
+                in0=y_tile[n][:, :, HALF:].rearrange("p t m -> p m t"),
+                scalar1=1.0,
+                scalar2=0.0,
+                op0=MULT,
+                op1=ADD,
+            )
 
-        def quantize_side(n):
-            if n < G_STEPS:
-                quantize_part(n, QUARTER - G_COLS, G_COLS, y_side[n])
+        def quantize_upper(n):
+            quantize_features(n, HALF, HALF, y_upper[n])
 
-        def interleave_y(n):
-            own = own_cols(n)
-            if own == 0:
-                return
-            y_grouped[n] = work.tile([P, own, PACK], BF16, name="y_grouped", bufs=4, align_bytes=64)
-            dst = y_grouped[n][:].rearrange("p (a i) t -> p a t i", i=4)
-            src = y_tile[n][:, :, :own].rearrange("p t (a i) -> p a t i", i=4)
-            cut = TAIL.get(n, 0) // 4
+        def round_lower(n, count, on_scalar):
+            y_lower[n] = work.tile([P, count, PACK], BF16, name="y_lower", bufs=4, align_bytes=64)
+            dst = y_lower[n][:].rearrange("p (a i) t -> p a t i", i=4)
+            src = y_tile[n][:, :, :count].rearrange("p t (a i) -> p a t i", i=4)
+            cut = on_scalar // 4
             if cut > 0:
                 nc.scalar.copy(out=dst[:, :cut], in_=src[:, :cut])
-            if cut < own // 4:
+            if on_scalar < count:
                 nc.vector.tensor_copy(out=dst[:, cut:], in_=src[:, cut:])
 
-        def quantize_y(n):
-            if own_cols(n) > 0:
-                quantize_part(n, 0, own_cols(n), y_grouped[n])
+        def quantize_lower(n):
+            quantize_features(n, 0, QUARTER if n == LAST else HALF, y_lower[n])
 
         def x_items(n):
             g, q = divmod(n, QUARTERS)
@@ -314,14 +310,23 @@ def tile_weighted_fourier_features_b14_kernel(tc, X_bytes, X_sbytes, X_rscale, W
         def w_items(n):
             return [(n + 2, c) for c in range(PASSES)] if 1 <= n + 2 < QUARTERS else []
 
+        def run(stage, n):
+            if 0 <= n < STEPS:
+                stage(n)
+
+        combine_scales(0)
         interleave_w(0, 0)
+        for item in range(PASSES):
+            widen_x(0, item, 0)
         for item in range(X_ITEMS):
-            widen_x(0, item)
+            if item >= PASSES:
+                widen_x(0, item, 0)
+            widen_x(0, item, 1)
             transpose_x(0, item)
             copy_out_x(0, item)
             if item == 1:
                 interleave_w(0, 1)
-            if item == 3:
+            if item == PASSES:
                 nc.scalar.copy(out=phase_f32[0:TILES, :], in_=phase_rows[:])
         interleave_w(0, 2)
         for c in range(PASSES):
@@ -329,83 +334,82 @@ def tile_weighted_fourier_features_b14_kernel(tc, X_bytes, X_sbytes, X_rscale, W
         for c in range(PASSES):
             quantize_x(0, c)
         make_phase_column()
+        combine_scales(1)
 
-        def run(stage, n):
-            if 0 <= n < STEPS:
-                stage(n)
-
-        last = STEPS - 1
-        round_slot = []
-        for n in range(STEPS - 3):
-            slot = max([n + Y_LAG] + round_slot[-1:])
-            while round_slot.count(slot) >= (ROOM2 if slot >= CATCH else ROOM[slot % QUARTERS]):
+        last_x_slot = QUARTERS * (GROUPS - 1) - 1
+        lower_slot = []
+        for n in range(STEPS - WEIGH_LAG):
+            slot = max([n + WEIGH_LAG] + lower_slot[-1:])
+            while lower_slot.count(slot) >= (2 if slot >= last_x_slot else 1 if slot % QUARTERS < 2 else 0):
                 slot += 1
-            round_slot.append(slot)
-        assert round_slot[-1] <= last
+            lower_slot.append(slot)
+
+        def lower_steps(slot):
+            return [n for n in range(len(lower_slot)) if lower_slot[n] == slot]
 
         for n in range(-1, STEPS):
+            weighed = n - WEIGH_LAG
             run(multiply, n)
             for item in x_items(n - 1):
                 copy_out_x(*item)
-            run(weigh, n - 3)
-            if not (EARLY and n == last):
+            run(weigh, weighed)
+            if n < LAST:
                 run(transpose_y, n - 2)
             for item in x_items(n):
                 transpose_x(*item)
             run(take_cosine, n - 1)
-            if EARLY and n >= last - 1:
-                run(transpose_y, n - 1)
-            for w in w_items(n - 1):
-                quantize_w(*w)
-            for m, slot in enumerate(round_slot):
-                if slot == n - 1:
-                    quantize_y(m)
+            if n >= LAST - 1:
+                transpose_y(n - 1)
+            for item in w_items(n - 1):
+                quantize_w(*item)
+            for m in lower_steps(n - 1):
+                quantize_lower(m)
+            if n == 0:
+                for g in range(2, GROUPS):
+                    combine_scales(g)
             run(fold, n)
-            for g, item in x_items(n - 1):
-                if item >= PASSES:
-                    quantize_x(g, item - PASSES)
-            for item in x_items(n + 1):
-                widen_x(*item)
-            for w in w_items(n):
-                interleave_w(*w)
-            rounds = [m for m, slot in enumerate(round_slot) if slot == n]
-            for m in rounds[:-1]:
-                interleave_y(m)
-            if n == 3:
-                round_side(0)
-            run(quantize_side, n - 4)
-            if n > 3:
-                run(round_side, n - 3)
-            for m in rounds[-1:]:
-                interleave_y(m)
+            ready = [(g, item - PASSES) for g, item in x_items(n - 1) if item >= PASSES]
+            closing = [(g, c) for g, c in ready if c == 0 and weighed > 0]
+            for g, c in ready:
+                if (g, c) not in closing:
+                    quantize_x(g, c)
+            for g, item in x_items(n + 1):
+                widen_x(g, item, 0)
+                widen_x(g, item, 1)
+            for item in w_items(n):
+                interleave_w(*item)
+            for m in lower_steps(n)[:-1]:
+                round_lower(m, HALF, 0)
+            run(quantize_upper, weighed - 1)
+            run(round_upper, weighed)
+            for m in lower_steps(n)[-1:]:
+                round_lower(m, HALF, 0)
+            for g, c in closing:
+                quantize_x(g, c)
 
-        take_cosine(last)
-        weigh(last - 2)
-        if EARLY:
-            for m, slot in enumerate(round_slot):
-                if slot == last:
-                    quantize_y(m)
-            quantize_side(last - 3)
-        round_side(last - 2)
-        if not EARLY:
-            transpose_y(last - 1)
-        weigh(last - 1)
-        transpose_y(last)
-        interleave_y(last - 2)
-        if EARLY:
-            quantize_side(last - 2)
-            quantize_y(last - 2)
-        round_side(last - 1)
-        weigh(last)
-        interleave_y(last - 1)
-        if not EARLY:
-            for m, slot in enumerate(round_slot):
-                if slot == last:
-                    quantize_y(m)
-            quantize_side(last - 3)
-            quantize_side(last - 2)
-            quantize_y(last - 2)
-        interleave_y(last)
-        quantize_side(last - 1)
-        quantize_y(last - 1)
-        quantize_y(last)
+        take_cosine(LAST)
+        weigh(LAST - 2)
+        for m in lower_steps(LAST):
+            quantize_lower(m)
+        quantize_upper(LAST - 3)
+        round_upper(LAST - 2)
+        weigh(LAST - 1)
+        round_upper(LAST - 1)
+        transpose_y(LAST)
+        round_lower(LAST - 2, HALF, HALF)
+        weigh(LAST)
+        round_lower(LAST - 1, HALF, HALF)
+        quantize_upper(LAST - 2)
+        quantize_lower(LAST - 2)
+        round_lower(LAST, QUARTER, LAST_ON_SCALAR)
+        quantize_upper(LAST - 1)
+        quantize_lower(LAST - 1)
+        quantize_lower(LAST)
+
+        scale_words = y_scales[:].bitcast(I32)
+        for quad in range(4):
+            queue = nc.scalar if quad % 2 else nc.sync
+            queue.dma_start(
+                out=y_scale_rows[:, PACK * quad : PACK * (quad + 1), :],
+                in_=scale_words[32 * quad : 32 * quad + PACK * GROUPS, :],
+            )

import math
from contextlib import ExitStack

import concourse.mybir as mybir
from concourse.masks import make_identity

T, K, D, B = 2048, 1536, 1024, 128
FLOPS = 2 * T * K * D

F32 = mybir.dt.float32
BF16 = mybir.dt.bfloat16
U32 = mybir.dt.uint32
I32 = mybir.dt.int32
U8 = mybir.dt.uint8
FP8 = mybir.dt.float8_e4m3fn
FP8X4 = mybir.dt.float8_e4m3fn_x4
ACT = mybir.ActivationFunctionType
MULT = mybir.AluOpType.mult
ADD = mybir.AluOpType.add

P = 128
PACK = 4
SPAN = P * PACK
GROUPS = T // SPAN
PASSES = K // SPAN
TILES = D // P
BLOCKS = K // B
QUARTER = 2 * P
QUARTERS = D // QUARTER
STEPS = GROUPS * QUARTERS
LAST = STEPS - 1
X_ITEMS = 2 * PASSES

U_BANKS = 3
T_BANKS = 5
WEIGH_LAG = 3
Y_BUFS = 10
HALF = QUARTER // 2
LAST_ON_SCALAR = 96


def tile_weighted_fourier_features_b14_kernel(tc, X_bytes, X_sbytes, X_rscale, W, phase, amp, root_w, out_0, out_1, out_2):
    nc = tc.nc
    x_rows = X_bytes.rearrange("(g p t) k -> g p t k", p=P, t=PACK)
    sbyte_rows = X_sbytes.rearrange("(g p t) b -> p g (t b)", p=P, t=PACK)
    rscale_rows = X_rscale.rearrange("(g p t) o -> p g (t o)", p=P, t=PACK)
    w_rows = W.rearrange("(c p j) n -> c p j n", p=P, j=PACK)
    y_rows = out_0.rearrange("(g p t) m -> g p t m", p=P, t=PACK)
    y_words = out_1.rearrange("g p m t -> g p (m t)").bitcast(I32)
    y_scale_rows = out_2.bitcast(I32)

    with ExitStack() as ctx:
        keep = ctx.enter_context(tc.tile_pool(name="keep", bufs=1))
        work = ctx.enter_context(tc.tile_pool(name="work", bufs=3))
        psum = ctx.enter_context(tc.psum_pool(name="psum", bufs=3))
        ctx.enter_context(tc.manual_schedule())

        sbytes, rscale, xbytes, w_raw = {}, {}, {}, {}

        def load_scales(first, count):
            codes = keep.tile([P, count, 64], U8, name="sbytes%d" % first)
            rows = keep.tile([P, count, 8], F32, name="rscale%d" % first)
            nc.sync.dma_start(out=codes[:, :, : PACK * BLOCKS], in_=sbyte_rows[:, first : first + count])
            nc.sync.dma_start(out=rows[:, :, :PACK], in_=rscale_rows[:, first : first + count])
            for i in range(count):
                sbytes[first + i] = codes[:, i, :]
                rscale[first + i] = rows[:, i, :]

        def load_x(g, first, count):
            rows = keep.tile([P, count, K], U8, name="xbytes%d_%d" % (g, first))
            nc.sync.dma_start(out=rows[:], in_=x_rows[g, :, first : first + count, :])
            for i in range(count):
                xbytes[g, first + i] = rows[:, i, :]

        def load_w(c, first, count):
            raw = keep.tile([P, PACK, count * QUARTER], BF16, name="wraw%d_%d" % (c, first))
            nc.sync.dma_start(out=raw[:], in_=w_rows[c, :, :, first * QUARTER : (first + count) * QUARTER])
            for i in range(count):
                w_raw[first + i, c] = raw[:, :, i * QUARTER : (i + 1) * QUARTER]

        rootw = keep.tile([P, GROUPS, PACK], BF16, name="rootw")
        phase_rows = keep.tile([TILES, P], BF16, name="phase_rows")
        amp_all = keep.tile([P, D], BF16, name="amp_all")

        load_scales(0, 1)
        load_x(0, 0, 1)
        load_w(0, 0, 1)
        load_x(0, 1, 1)
        load_x(0, 2, 2)
        load_w(1, 0, 1)
        load_w(2, 0, 1)
        nc.sync.dma_start(out=phase_rows[:], in_=phase.rearrange("o (j p) -> (o j) p", p=P))
        load_scales(1, GROUPS - 1)
        for c in range(PASSES):
            load_w(c, 1, 1)
        load_x(1, 0, 2)
        load_w(0, 2, 2)
        load_x(1, 2, 2)
        load_w(1, 2, 2)
        load_w(2, 2, 2)
        nc.sync.dma_start(out=rootw[:], in_=root_w.rearrange("(g p t) o -> p g (t o)", p=P, t=PACK))
        nc.sync.dma_start(out=amp_all[:], in_=amp.rearrange("o n -> (o n)").partition_broadcast(P))
        for g in range(2, GROUPS):
            load_x(g, 0, 2)
            load_x(g, 2, 2)

        ident = keep.tile([P, P], F32, name="ident")
        make_identity(nc, ident[:])
        phase_f32 = keep.tile([P, P], F32, name="phase_f32")
        nc.gpsimd.memset(phase_f32[:], 0.0)
        table_preload = keep.tile([P, 1], F32, name="table_preload")
        nc.scalar.activation(out=table_preload[:], in_=phase_f32[:, 0:1], func=ACT.Sin)

        xscale = keep.tile([P, GROUPS * PACK, BLOCKS], F32, name="xscale")
        phase_col = keep.tile([P, TILES], F32, name="phase_col")

        def combine_scales(g):
            for t in range(PACK):
                nc.scalar.activation(
                    out=xscale[:, PACK * g + t, :],
                    in_=sbytes[g][:, t * BLOCKS : (t + 1) * BLOCKS].bitcast(FP8),
                    func=ACT.Copy,
                    scale=rscale[g][:, t : t + 1],
                )

        def make_phase_column():
            bank = psum.tile([P, P], F32, name="phase_bank", tag="t_bank", bufs=T_BANKS)
            nc.tensor.transpose(out=bank[:], in_=phase_f32[:], identity=ident[:])
            nc.scalar.copy(out=phase_col[:], in_=bank[:, 0:TILES])

        w_grouped, w_codes, w_scales = {}, {}, {}

        def interleave_w(q, c):
            w_grouped[q, c] = work.tile([P, QUARTER, PACK], BF16, name="w_grouped", bufs=4, align_bytes=64)
            dst = w_grouped[q, c][:].rearrange("p (a i) j -> p a j i", i=4)
            src = w_raw[q, c].rearrange("p j (a i) -> p a j i", i=4)
            if c == 0 or (q, c) == (0, 1):
                nc.scalar.copy(out=dst, in_=src)
            else:
                nc.vector.tensor_copy(out=dst, in_=src)

        def quantize_w(q, c):
            w_codes[q, c] = keep.tile([P, QUARTER], U32, name="wcodes%d_%d" % (q, c), align_bytes=64)
            w_scales[q, c] = keep.tile([P, QUARTER], U8, name="wscales%d_%d" % (q, c), align_bytes=64)
            nc.vector.quantize_mx(
                out=w_codes[q, c][:].bitcast(FP8X4),
                scales=w_scales[q, c][:],
                in_=w_grouped[q, c][:].rearrange("p n j -> p (n j)"),
            )

        x_wide, x_bank, x_grouped, x_codes, x_scales = {}, {}, {}, {}, {}

        def widen_x(g, item, tt):
            pair, c = divmod(item, PASSES)
            if tt == 0:
                x_wide[g, item] = work.tile([P, 2, SPAN], BF16, name="x_wide", bufs=5)
            sorted_view = x_wide[g, item][:, tt, :].rearrange("r (u p e) -> r p u e", u=2, e=2)
            for b in range(SPAN // B):
                block = c * (SPAN // B) + b
                src = xbytes[g, 2 * pair + tt][:, block * B : (block + 1) * B].bitcast(FP8)
                nc.vector.tensor_scalar(
                    out=sorted_view[:, (B // PACK) * b : (B // PACK) * (b + 1)],
                    in0=src.rearrange("r (p u e) -> r p u e", u=2, e=2),
                    scalar1=xscale[:, PACK * g + 2 * pair + tt, block : block + 1],
                    scalar2=None,
                    op0=MULT,
                )

        def transpose_x(g, item):
            x_bank[g, item] = psum.tile([P, 2, 2, P], F32, name="x_bank", tag="t_bank", bufs=T_BANKS)
            words = x_wide[g, item][:].rearrange("r t k -> r (t k)").bitcast(F32)
            for tt in range(2):
                for u in range(2):
                    first = (2 * tt + u) * P
                    nc.tensor.transpose(out=x_bank[g, item][:, tt, u, :], in_=words[:, first : first + P], identity=ident[:])

        def copy_out_x(g, item):
            pair, c = divmod(item, PASSES)
            if pair == 0:
                x_grouped[g, c] = work.tile([P, SPAN, 2], F32, name="x_grouped", bufs=4, align_bytes=64)
            dst = x_grouped[g, c][:, 2 * P * pair : 2 * P * (pair + 1), :].rearrange("p (t r) u -> p t r u", t=2)
            nc.scalar.copy(out=dst, in_=x_bank[g, item][:].rearrange("p t u r -> p t r u"))

        def quantize_x(g, c):
            x_codes[g, c] = work.tile([P, SPAN], U32, name="x_codes", bufs=2 * PASSES + 1, align_bytes=64)
            x_scales[g, c] = work.tile([P, SPAN], U8, name="x_scales", bufs=2 * PASSES + 1, align_bytes=64)
            nc.vector.quantize_mx(
                out=x_codes[g, c][:].bitcast(FP8X4),
                scales=x_scales[g, c][:],
                in_=x_grouped[g, c][:].rearrange("p r u -> p (r u)").bitcast(BF16),
            )

        u_bank, folded, cosine, y_bank, y_tile = {}, {}, {}, {}, {}
        whole = [slice(0, SPAN)]
        by_pair = [slice(0, SPAN // 2), slice(SPAN // 2, SPAN)]

        def multiply(n):
            g, q = divmod(n, QUARTERS)
            for j in range(2):
                cols = slice(j * P, (j + 1) * P)
                u_bank[n, j] = psum.tile([P, SPAN], F32, name="u_bank", bufs=U_BANKS)
                for c in range(PASSES):
                    nc.tensor.matmul_mx(
                        out=u_bank[n, j][:],
                        lhsT=w_codes[q, c][:, cols].bitcast(FP8X4),
                        lhsT_scale=w_scales[q, c][:, cols],
                        rhs=x_codes[g, c][:].bitcast(FP8X4),
                        rhs_scale=x_scales[g, c][:],
                        start=(c == 0),
                        stop=(c == PASSES - 1),
                    )

        def fold(n):
            folded[n] = work.tile([P, 2, SPAN], F32, name="folded", bufs=2)
            for j in range(2):
                tile = 2 * (n % QUARTERS) + j
                for part in by_pair if (n, j) == (LAST, 1) else whole:
                    nc.scalar.activation(out=folded[n][:, j, part], in_=u_bank[n, j][:, part], func=ACT.Abs, bias=phase_col[:, tile : tile + 1])

        def take_cosine(n):
            cosine[n] = work.tile([P, 2, SPAN], F32, name="cosine")
            if n == LAST:
                pieces = [(slice(0, 2), part) for part in by_pair]
            elif x_items(n):
                pieces = [(slice(0, 2), slice(0, SPAN))]
            else:
                pieces = [(slice(j, j + 1), slice(0, SPAN)) for j in range(2)]
            for tiles, part in pieces:
                nc.scalar.activation(out=cosine[n][:, tiles, part], in_=folded[n][:, tiles, part], func=ACT.Sin, scale=-1.0, bias=math.pi / 2)

        def transpose_y(n):
            for pair in range(2):
                y_bank[n, pair] = psum.tile([P, 2, 2, P], F32, name="y_bank", tag="t_bank", bufs=T_BANKS)
                for tt in range(2):
                    t = 2 * pair + tt
                    for j in range(2):
                        nc.tensor.transpose(out=y_bank[n, pair][:, tt, j, :], in_=cosine[n][:, j, t * P : (t + 1) * P], identity=ident[:])

        def weigh(n):
            g, q = divmod(n, QUARTERS)
            cols = slice(q * QUARTER, (q + 1) * QUARTER)
            y_tile[n] = work.tile([P, PACK, QUARTER], F32, name="y_tile", bufs=Y_BUFS)
            for pair in range(2):
                for tt in range(2):
                    t = 2 * pair + tt
                    nc.vector.scalar_tensor_tensor(
                        out=y_tile[n][:, t, :],
                        in0=y_bank[n, pair][:, tt].rearrange("p j m -> p (j m)"),
                        scalar=rootw[:, g, t : t + 1],
                        in1=amp_all[:, cols],
                        op0=MULT,
                        op1=MULT,
                    )
                if n == LAST:
                    rows = slice(2 * pair, 2 * pair + 2)
                    nc.sync.dma_start(out=y_rows[g, :, rows, cols], in_=y_tile[n][:, rows, :])
            if n < LAST:
                nc.sync.dma_start(out=y_rows[g, :, :, cols], in_=y_tile[n][:])

        y_scales = keep.tile([P, D], U8, name="y_scales", align_bytes=64)
        y_lower, y_upper, y_codes, features_left = {}, {}, {}, {}

        def quantize_features(n, first, count, rounded):
            g, q = divmod(n, QUARTERS)
            if n not in y_codes:
                y_codes[n] = work.tile([P, QUARTER], U32, name="y_codes", bufs=Y_BUFS, align_bytes=64)
                features_left[n] = QUARTER
            nc.vector.quantize_mx(
                out=y_codes[n][:, first : first + count].bitcast(FP8X4),
                scales=y_scales[PACK * g :, q * QUARTER + first : q * QUARTER + first + count],
                in_=rounded[:].rearrange("p m t -> p (m t)"),
            )
            features_left[n] = features_left[n] - count
            if features_left[n] == 0:
                nc.sync.dma_start(out=y_words[g, :, q * QUARTER : (q + 1) * QUARTER], in_=y_codes[n][:].bitcast(I32))

        def round_upper(n):
            name = "y_upper" if n < LAST - 1 else "y_upper_end"
            y_upper[n] = work.tile([P, HALF, PACK], BF16, name=name, bufs=1, align_bytes=64)
            engine = nc.gpsimd if n > 0 else nc.vector
            engine.tensor_scalar(
                out=y_upper[n][:],
                in0=y_tile[n][:, :, HALF:].rearrange("p t m -> p m t"),
                scalar1=1.0,
                scalar2=0.0,
                op0=MULT,
                op1=ADD,
            )

        def quantize_upper(n):
            quantize_features(n, HALF, HALF, y_upper[n])

        def round_lower(n, count, on_scalar):
            y_lower[n] = work.tile([P, count, PACK], BF16, name="y_lower", bufs=4, align_bytes=64)
            dst = y_lower[n][:].rearrange("p (a i) t -> p a t i", i=4)
            src = y_tile[n][:, :, :count].rearrange("p t (a i) -> p a t i", i=4)
            cut = on_scalar // 4
            if cut > 0:
                nc.scalar.copy(out=dst[:, :cut], in_=src[:, :cut])
            if on_scalar < count:
                nc.vector.tensor_copy(out=dst[:, cut:], in_=src[:, cut:])

        def quantize_lower(n):
            quantize_features(n, 0, QUARTER if n == LAST else HALF, y_lower[n])

        def x_items(n):
            g, q = divmod(n, QUARTERS)
            return [(g + 1, 2 * q), (g + 1, 2 * q + 1)] if 0 <= g < GROUPS - 1 and q < PASSES else []

        def w_items(n):
            return [(n + 2, c) for c in range(PASSES)] if 1 <= n + 2 < QUARTERS else []

        def run(stage, n):
            if 0 <= n < STEPS:
                stage(n)

        combine_scales(0)
        interleave_w(0, 0)
        for item in range(PASSES):
            widen_x(0, item, 0)
        for item in range(X_ITEMS):
            if item >= PASSES:
                widen_x(0, item, 0)
            widen_x(0, item, 1)
            transpose_x(0, item)
            copy_out_x(0, item)
            if item == 1:
                interleave_w(0, 1)
            if item == PASSES:
                nc.scalar.copy(out=phase_f32[0:TILES, :], in_=phase_rows[:])
        interleave_w(0, 2)
        for c in range(PASSES):
            quantize_w(0, c)
        for c in range(PASSES):
            quantize_x(0, c)
        make_phase_column()
        combine_scales(1)

        last_x_slot = QUARTERS * (GROUPS - 1) - 1
        lower_slot = []
        for n in range(STEPS - WEIGH_LAG):
            slot = max([n + WEIGH_LAG] + lower_slot[-1:])
            while lower_slot.count(slot) >= (2 if slot >= last_x_slot else 1 if slot % QUARTERS < 2 else 0):
                slot += 1
            lower_slot.append(slot)

        def lower_steps(slot):
            return [n for n in range(len(lower_slot)) if lower_slot[n] == slot]

        for n in range(-1, STEPS):
            weighed = n - WEIGH_LAG
            run(multiply, n)
            for item in x_items(n - 1):
                copy_out_x(*item)
            run(weigh, weighed)
            if n < LAST:
                run(transpose_y, n - 2)
            for item in x_items(n):
                transpose_x(*item)
            run(take_cosine, n - 1)
            if n >= LAST - 1:
                transpose_y(n - 1)
            for item in w_items(n - 1):
                quantize_w(*item)
            for m in lower_steps(n - 1):
                quantize_lower(m)
            if n == 0:
                for g in range(2, GROUPS):
                    combine_scales(g)
            run(fold, n)
            ready = [(g, item - PASSES) for g, item in x_items(n - 1) if item >= PASSES]
            closing = [(g, c) for g, c in ready if c == 0 and weighed > 0]
            for g, c in ready:
                if (g, c) not in closing:
                    quantize_x(g, c)
            for g, item in x_items(n + 1):
                widen_x(g, item, 0)
                widen_x(g, item, 1)
            for item in w_items(n):
                interleave_w(*item)
            for m in lower_steps(n)[:-1]:
                round_lower(m, HALF, 0)
            run(quantize_upper, weighed - 1)
            run(round_upper, weighed)
            for m in lower_steps(n)[-1:]:
                round_lower(m, HALF, 0)
            for g, c in closing:
                quantize_x(g, c)

        take_cosine(LAST)
        weigh(LAST - 2)
        for m in lower_steps(LAST):
            quantize_lower(m)
        quantize_upper(LAST - 3)
        round_upper(LAST - 2)
        weigh(LAST - 1)
        round_upper(LAST - 1)
        transpose_y(LAST)
        round_lower(LAST - 2, HALF, HALF)
        weigh(LAST)
        round_lower(LAST - 1, HALF, HALF)
        quantize_upper(LAST - 2)
        quantize_lower(LAST - 2)
        round_lower(LAST, QUARTER, LAST_ON_SCALAR)
        quantize_upper(LAST - 1)
        quantize_lower(LAST - 1)
        quantize_lower(LAST)

        scale_words = y_scales[:].bitcast(I32)
        for quad in range(4):
            queue = nc.scalar if quad % 2 else nc.sync
            queue.dma_start(
                out=y_scale_rows[:, PACK * quad : PACK * (quad + 1), :],
                in_=scale_words[32 * quad : 32 * quad + PACK * GROUPS, :],
            )
